import numpy as np
CORES = [0,1,2,3,4,5,6,7]
N = 8
H = 2
PERIODIC = True
def setup_inputs(rng):
    return {"x": rng.standard_normal((N, 128, 4096), dtype=np.float32)}
def reference(x):
    W = x.shape[2]
    y = np.zeros((N, 128, W + 2 * H), x.dtype)
    for r in range(N):
        y[r][:, H:H + W] = x[r]
        left, right = r - 1, r + 1
        if PERIODIC:
            left, right = left % N, right % N
        if 0 <= left < N:
            y[r][:, :H] = x[left][:, W - H:]
        if 0 <= right < N:
            y[r][:, W + H:] = x[right][:, :H]
    return {"y": y}

from concourse.bass import DstId, RemoteDMATransfer

H = 2

SCRATCH = {
    "edge": ("sbuf", [128, 2 * H], "float32"),
    "land": ("sbuf", [128, 2 * H], "float32"),
}
SEMAPHORES = ["loaded", "sent", "arrived", "stored"]

LO_ENGINES = 0x00FF
HI_ENGINES = 0xFF00


def rank_program(g, core, T, topo):
    rank = T.rank_of(core)
    if rank is None:
        return
    n = len(T.cores)
    w = T.x.shape[1]
    left = T.cores[(rank - 1) % n]
    right = T.cores[(rank + 1) % n]

    g.sync.dma_start(T.edge[:, 0:H], T.x[:, 0:H]).then_inc(T.sem.loaded, 16)
    g.scalar.dma_start(T.edge[:, H:2 * H], T.x[:, w - H:w]).then_inc(T.sem.loaded, 16)

    g.sync.dma_start(T.y[:, H:H + w], T.x[:, :]).then_inc(T.sem.stored, 16)

    g.wait_ge(T.sem.loaded, 32)
    l_rid, l_pid, _l = topo.addr(left)
    r_rid, r_pid, _r = topo.addr(right)
    g.remote_dma_fused(
        [
            RemoteDMATransfer(
                dst_ids=[DstId(rid=l_rid, pnc=l_pid)],
                dma_engine_mask=LO_ENGINES,
                remote_sem=T.sem.arrived,
                src=T.edge[:, 0:H],
                dst=T.land[:, H:2 * H],
            ),
            RemoteDMATransfer(
                dst_ids=[DstId(rid=r_rid, pnc=r_pid)],
                dma_engine_mask=HI_ENGINES,
                remote_sem=T.sem.arrived,
                src=T.edge[:, H:2 * H],
                dst=T.land[:, 0:H],
            ),
        ],
        local_sem=T.sem.sent,
    )

    g.scalar.wait_ge(T.sem.arrived, 16)
    g.scalar.dma_start(T.y[:, 0:H], T.land[:, 0:H]).then_inc(T.sem.stored, 16)
    g.scalar.dma_start(T.y[:, H + w:2 * H + w], T.land[:, H:2 * H]).then_inc(T.sem.stored, 16)

    g.wait_ge(T.sem.sent, 16)
    g.wait_ge(T.sem.stored, 48)
